import numpy as np
import ml_dtypes


def mxq(x, axis, fmt="e4m3"):
    dtype, down = {"e4m3": (ml_dtypes.float8_e4m3fn, 7), "e5m2": (ml_dtypes.float8_e5m2, 14)}[fmt]
    v = np.moveaxis(np.asarray(x, np.float32).astype(ml_dtypes.bfloat16).astype(np.float64), axis, -1)
    blocks = v.reshape(v.shape[:-1] + (-1, 32))
    amax = np.abs(blocks).max(-1, keepdims=True)
    byte = np.maximum(np.where(amax > 0, np.frexp(amax)[1] - 1 + 127, 0) - down, 1)
    scale = np.exp2(byte - 127.0)
    codes = (blocks / scale).astype(np.float32).astype(dtype).astype(np.float64)
    return np.moveaxis((codes * scale).reshape(v.shape), -1, axis)


WIDE = False


def mx_kscale(k):
    if not WIDE:
        return np.ones(k)
    levels = np.array([10, -10, 5, -5, 0])
    if k % 512:
        return np.exp2(np.random.permutation(np.resize(levels, k // 32))).repeat(32)
    a = np.empty((k // 512, 16))
    for p in range(k // 512):
        a[p, :8] = np.random.permutation(np.resize(levels, 8))
        for g in range(8):
            far = levels[np.abs(levels - a[p, g]) >= 10]
            a[p, g + 8] = far[np.random.randint(len(far))]
    return np.exp2(a.ravel()).repeat(32)


def f64(x):
    return np.asarray(x).astype(np.float64)


def striped(idx):
    return np.tile(idx.reshape(-1, 16).T, (8, 1)).astype(np.uint16)


def unstriped(offs):
    return offs[:16].T.reshape(-1).astype(np.int64)


def striped8(idx):
    return np.concatenate([x.reshape(-1, 16).T for x in idx]).astype(np.uint16)


def runs(offs, k):
    lists = np.stack([offs[16 * r : 16 * r + 16].T.reshape(-1) for r in range(8)]).astype(np.int64)
    return lists[np.arange(k) % 512 // 64]


def pack_weight(w):
    k, n = w.shape
    w = f64(np.asarray(w, np.float32).astype(ml_dtypes.bfloat16)).reshape(k // 32, 32, n)
    amax = np.abs(w).max(1)
    byte = np.clip(np.where(amax > 0, np.frexp(amax)[1] - 1 + 127 - 7, 1), 1, 254)
    scaled = (w * np.exp2(127.0 - byte)[:, None, :]).reshape(k, n).astype(np.float32)
    words = np.ascontiguousarray(scaled.reshape(k // 512, 128, 4, n).transpose(0, 1, 3, 2)).astype(ml_dtypes.float8_e4m3fn).view(np.uint8)
    return words, np.ascontiguousarray(byte.astype(np.uint8).reshape(k // 512, 16, n))


def unpack_weight(words, scales):
    g, p, n, _ = words.shape
    vals = np.ascontiguousarray(words).view(ml_dtypes.float8_e4m3fn).astype(np.float64) * np.repeat(np.exp2(scales.astype(np.float64) - 127.0), 8, axis=1)[..., None]
    return vals.transpose(0, 1, 3, 2).reshape(g * 512, n)


K, T, S, N, H = 512, 2048, 512, 512, 512


def setup_inputs():
    n = np.random.standard_normal
    s = mx_kscale(K)[:, None]
    u = mx_kscale(H)
    packed_xT = pack_weight(n((K, T)) * s)
    return {
        "x_words": packed_xT[0],
        "x_scales": packed_xT[1],
        "w1": (n((K, H)) / np.sqrt(K) / s).astype(np.float32),
        "w2": (n((K, H)) / np.sqrt(K) / s).astype(np.float32),
        "gn": (np.random.uniform(0.5, 1.5, (H, 1)) * u[:, None]).astype(np.float32),
        "w3": (n((H, N)) / np.sqrt(H) / u[:, None]).astype(np.float32),
        "offs": striped(np.random.permutation(T)[:S]),
        "two": striped(np.random.permutation(T)[:S]),
        "n1": striped8(np.stack([np.random.permutation(S) for _ in range(8)])),
        "n2": striped8(np.stack([np.random.permutation(S) for _ in range(8)])),
        "n3": striped8(np.stack([np.random.permutation(S) for _ in range(8)])),
        "n4": striped8(np.stack([np.random.permutation(S) for _ in range(8)])),
        "n5": striped8(np.stack([np.random.permutation(S) for _ in range(8)])),
        "n6": striped8(np.stack([np.random.permutation(S) for _ in range(8)])),
    }


def reference(x_words, x_scales, w1, w2, gn, w3, offs, two, n1, n2, n3, n4, n5, n6):
    xq = unpack_weight(x_words, x_scales)[:, unstriped(offs)]
    y = mxq(f64(w1), 0, "e4m3").T @ xq
    x_two = unpack_weight(x_words, x_scales)[:, unstriped(two)]
    d = mxq(f64(w2), 0, "e4m3").T @ x_two
    z = f64(gn) * (np.maximum(y[np.arange(H)[:, None], runs(n1, H)] + d[np.arange(H)[:, None], runs(n3, H)], y[np.arange(H)[:, None], runs(n2, H)] + d[np.arange(H)[:, None], runs(n4, H)]))
    h = mxq(f64(w3), 0, "e4m3").T @ mxq(z, 0, "e4m3")
    st = np.maximum(h, h[np.arange(N)[:, None], runs(n5, N)])
    return np.minimum(st, st[np.arange(N)[:, None], runs(n6, N)])

@@ -1,0 +1,205 @@
+from contextlib import ExitStack
+
+import concourse.mybir as mybir
+
+F32 = mybir.dt.float32
+BF16 = mybir.dt.bfloat16
+I32 = mybir.dt.int32
+U32 = mybir.dt.uint32
+U16 = mybir.dt.uint16
+U8 = mybir.dt.uint8
+FP8X4 = mybir.dt.float8_e4m3fn_x4
+ALU = mybir.AluOpType
+COPY = mybir.ActivationFunctionType.Copy
+
+P = 128
+PACK = 4
+T = 2048
+S = 512
+F = 512
+WINDOW = 2 * S
+Z_CHUNKS = ((0, 256), (256, 384), (384, 512))
+FLOPS = 3 * 2 * F * F * S
+
+
+def tile_picked_twlpathbhopmn_none_p_kernel(
+    tc, x_words, x_scales, w1, w2, gn, w3, offs, two, n1, n2, n3, n4, n5, n6, out
+):
+    nc = tc.nc
+    with ExitStack() as ctx:
+        keep = ctx.enter_context(tc.tile_pool(name="keep", bufs=1))
+        psum = ctx.enter_context(tc.psum_pool(name="psum", bufs=1))
+
+        def load_list(name, source):
+            tile = keep.tile([P, S // 16], U16, name=name)
+            nc.sync.dma_start(tile[:], source)
+            return tile
+
+        def load_weight(name, source, c0, c1):
+            tile = keep.tile([P, PACK, c1 - c0], F32, name=name)
+            nc.sync.dma_start(tile[:], source.rearrange("(p j) c -> p j c", j=PACK)[:, :, c0:c1])
+            return tile
+
+        def deal(grouped, rows, m0, m1, copy=nc.scalar.copy):
+            copy(
+                out=grouped[:].rearrange("p (t m j) -> p m j t", t=PACK, j=PACK)[:, m0:m1],
+                in_=rows.rearrange("p j (m t) -> p m j t", t=PACK),
+            )
+
+        def quantise(name, grouped, width):
+            codes = keep.tile([P, width], U32, name=name + "_codes", align_bytes=64)
+            scales = keep.tile([P, width], U8, name=name + "_scales", align_bytes=64)
+            nc.vector.quantize_mx(out=codes[:].bitcast(FP8X4), scales=scales[:], in_=grouped[:])
+            return codes, scales
+
+        def product(acc, weight, t, moving):
+            cols = slice(P * t, P * (t + 1))
+            nc.tensor.matmul_mx(
+                out=acc,
+                lhsT=weight[0][:, cols].bitcast(FP8X4),
+                lhsT_scale=weight[1][:, cols],
+                rhs=moving[0][:].bitcast(FP8X4),
+                rhs_scale=moving[1][:],
+                start=True,
+                stop=True,
+            )
+
+        scale_table = keep.tile([P, T], U8, name="scale_table")
+        nc.vector.memset(scale_table[:].bitcast(I32), 0)
+        offs_t = load_list("offs_t", offs)
+        two_t = load_list("two_t", two)
+        half = F // 2
+        w1_left = load_weight("w1_left", w1, 0, half)
+        for q in range(4):
+            nc.sync.dma_start(
+                scale_table[32 * q : 32 * q + 4, :].bitcast(I32), x_scales[0, 4 * q : 4 * q + 4, :].bitcast(I32)
+            )
+        w1_right = load_weight("w1_right", w1, half, F)
+        word_table = keep.tile([P, T], U32, name="word_table")
+        nc.sync.dma_start(word_table[:].bitcast(I32), x_words[0].rearrange("p n t -> p (n t)").bitcast(I32))
+        gain = keep.tile([P, PACK], F32, name="gain")
+        nc.gpsimd.dma_start(gain[:], gn.rearrange("(p t) o -> p (t o)", t=PACK))
+        n1_t = load_list("n1_t", n1)
+        n2_t = load_list("n2_t", n2)
+        w2_rows = load_weight("w2_rows", w2, 0, F)
+        n3_t = load_list("n3_t", n3)
+        n4_t = load_list("n4_t", n4)
+        w3_rows = load_weight("w3_rows", w3, 0, F)
+        n5_t = load_list("n5_t", n5)
+        n6_t = load_list("n6_t", n6)
+
+        first = [keep.tile([P, WINDOW], F32, name="first%d" % t) for t in range(PACK)]
+        second = [keep.tile([P, WINDOW], F32, name="second%d" % t) for t in range(PACK)]
+        nc.vector.memset(first[0][:, S:], 0.0)
+        for t in range(1, PACK):
+            nc.scalar.activation(first[t][:, S:], first[0][:, S:], COPY)
+        for t in range(PACK):
+            nc.vector.memset(second[t][:, S:], 0.0)
+
+        sign = keep.tile([P, PACK], F32, name="sign")
+        twice = keep.tile([P, PACK], F32, name="twice")
+        size = keep.tile([P, PACK], F32, name="size")
+        nc.vector.tensor_scalar(twice[:], gain[:], 0.0, 2.0, ALU.is_ge, ALU.mult)
+        nc.vector.tensor_scalar(sign[:], twice[:], -1.0, None, ALU.add)
+        nc.vector.tensor_tensor(size[:], gain[:], sign[:], ALU.mult)
+
+        picked = []
+        for name, lst in (("x_offs", offs_t), ("x_two", two_t)):
+            scales = keep.tile([P, S], U8, name=name + "_scales", align_bytes=64)
+            nc.vector.tensor_copy(scales[:], scale_table[:].indirect(lst[:]))
+            picked.append(scales)
+
+        w1_grouped = keep.tile([P, PACK * F], BF16, name="w1_grouped", align_bytes=64)
+        deal(w1_grouped, w1_left[:], 0, 64)
+        deal(w1_grouped, w1_right[:], 64, 128)
+        w1_q = quantise("w1", w1_grouped, F)
+
+        tokens = []
+        for name, lst, scales in (("x_offs", offs_t, picked[0]), ("x_two", two_t, picked[1])):
+            words = keep.tile([P, S], U32, name=name + "_words", align_bytes=64)
+            nc.vector.tensor_copy(words[:], word_table[:].indirect(lst[:]))
+            tokens.append((words, scales))
+
+        banks = [psum.tile([P, S], F32, name="bank%d" % b) for b in range(2 * PACK)]
+
+        for t in range(PACK):
+            product(banks[t][:], w1_q, t, tokens[0])
+            nc.scalar.activation(first[t][:, :S], banks[t][:], COPY, scale=size[:, t : t + 1])
+
+        w2_grouped = keep.tile([P, PACK * F], BF16, name="w2_grouped", tag="w2_stage", align_bytes=64)
+        for h in range(2):
+            deal(w2_grouped, w2_rows[:, :, half * h : half * (h + 1)], 64 * h, 64 * (h + 1))
+
+        y_n1 = keep.tile([P, PACK, S], F32, name="y_n1")
+        y_n2_early = keep.tile([P, 2, S], F32, name="y_n2_early")
+        for t in range(PACK):
+            nc.vector.tensor_copy(y_n1[:, t, :], first[t][:].indirect(n1_t[:]))
+            if t < 2:
+                nc.vector.tensor_copy(y_n2_early[:, t, :], first[t][:].indirect(n2_t[:]))
+        w2_q = quantise("w2", w2_grouped, F)
+        y_n2_late = keep.tile([P, 2, S], F32, name="y_n2_late", tag="w2_stage", align_bytes=64)
+        for t in range(2, PACK):
+            nc.vector.tensor_copy(y_n2_late[:, t - 2, :], first[t][:].indirect(n2_t[:]))
+        y_n2 = [y_n2_early[:, 0, :], y_n2_early[:, 1, :], y_n2_late[:, 0, :], y_n2_late[:, 1, :]]
+
+        for t in range(PACK):
+            product(banks[PACK + t][:], w2_q, t, tokens[1])
+            nc.scalar.activation(second[t][:, :S], banks[PACK + t][:], COPY, scale=size[:, t : t + 1])
+
+        w3_signed = keep.tile([P, PACK, F], BF16, name="w3_signed")
+        for j in range(PACK):
+            nc.scalar.activation(w3_signed[:, j, :], w3_rows[:, j, :], COPY, scale=sign[:, j : j + 1])
+        w3_grouped = keep.tile([P, PACK * F], BF16, name="w3_grouped", align_bytes=64)
+        for h in range(2):
+            deal(w3_grouped, w3_signed[:, :, half * h : half * (h + 1)], 64 * h, 64 * (h + 1))
+
+        sum_a = keep.tile([P, PACK, S], F32, name="sum_a")
+        sum_b = keep.tile([P, PACK, S], F32, name="sum_b")
+        for t in range(PACK):
+            nc.vector.tensor_tensor(sum_a[:, t, :], second[t][:].indirect(n3_t[:]), y_n1[:, t, :], ALU.add)
+            nc.vector.tensor_tensor(sum_b[:, t, :], second[t][:].indirect(n4_t[:]), y_n2[t], ALU.add)
+        w3_q = quantise("w3", w3_grouped, F)
+
+        z_grouped = []
+        for c0, c1 in Z_CHUNKS:
+            grouped = keep.tile([P, PACK * (c1 - c0)], BF16, name="z_grouped%d" % c0, align_bytes=64)
+            nc.vector.tensor_tensor(
+                grouped[:].rearrange("p (c i t) -> p c t i", i=4, t=PACK),
+                sum_a[:, :, c0:c1].rearrange("p t (c i) -> p c t i", i=4),
+                sum_b[:, :, c0:c1].rearrange("p t (c i) -> p c t i", i=4),
+                ALU.max,
+            )
+            z_grouped.append(grouped)
+        last0 = Z_CHUNKS[-1][0]
+        for grouped, (c0, c1) in zip(z_grouped, Z_CHUNKS):
+            z_q = quantise("z%d" % c0, grouped, c1 - c0)
+            for t in range(PACK):
+                bank = banks[t] if c0 < last0 else banks[PACK + t]
+                product(bank[:, c0:c1], w3_q, t, z_q)
+                if c1 == last0:
+                    nc.scalar.copy(first[t][:, :last0], bank[:, :last0])
+                if c0 == last0:
+                    nc.scalar.copy(first[t][:, last0:S], bank[:, last0:S])
+
+        out_rows = out.rearrange("(p t) j -> p t j", t=PACK)
+        h_n5 = [keep.tile([P, S], F32, name="h_n5_%d" % t) for t in range(PACK)]
+        for t in range(PACK):
+            nc.vector.tensor_copy(h_n5[t][:], first[t][:].indirect(n5_t[:]))
+            if t > 0:
+                nc.vector.tensor_tensor(second[t - 1][:, :S], h_n5[t - 1][:], first[t - 1][:, :S], ALU.max)
+        pieces = [(t, 0, S) for t in range(PACK - 1)] + [(PACK - 1, 0, S // 2), (PACK - 1, S // 2, S)]
+        fetched = []
+        for n, (t, c0, c1) in enumerate(pieces):
+            st_n6 = keep.tile([P, c1 - c0], F32, name="st_n6_%d" % n)
+            nc.vector.tensor_copy(st_n6[:], second[t][:].indirect(n6_t[:, c0 // 16 : c1 // 16]))
+            fetched.append(st_n6)
+            if n == 0:
+                nc.vector.tensor_tensor(second[PACK - 1][:, :S], h_n5[PACK - 1][:], first[PACK - 1][:, :S], ALU.max)
+            todo = [n - 1] if n > 0 else []
+            if n == len(pieces) - 1:
+                todo.append(n)
+            for k in todo:
+                tk, k0, k1 = pieces[k]
+                result = keep.tile([P, k1 - k0], F32, name="result%d" % k)
+                nc.vector.tensor_tensor(result[:], fetched[k][:], second[tk][:, k0:k1], ALU.min)
+                nc.sync.dma_start(out_rows[:, tk, k0:k1], result[:])

@@ -40,10 +40,10 @@ def tile_picked_twlpathbhopmn_none_p_kernel(
             nc.sync.dma_start(tile[:], source.rearrange("(p j) c -> p j c", j=PACK)[:, :, c0:c1])
             return tile
 
-        def deal(grouped, rows, m0, m1, copy=nc.scalar.copy):
-            copy(
-                out=grouped[:].rearrange("p (t m j) -> p m j t", t=PACK, j=PACK)[:, m0:m1],
-                in_=rows.rearrange("p j (m t) -> p m j t", t=PACK),
+        def deal(grouped, rows, m0, m1):
+            nc.scalar.copy(
+                out=grouped[:].rearrange("p (t m j) -> p m t j", t=PACK, j=PACK)[:, m0:m1],
+                in_=rows.rearrange("p j (m t) -> p m t j", t=PACK),
             )
 
         def quantise(name, grouped, width):
@@ -75,10 +75,10 @@ def tile_picked_twlpathbhopmn_none_p_kernel(
                 scale_table[32 * q : 32 * q + 4, :].bitcast(I32), x_scales[0, 4 * q : 4 * q + 4, :].bitcast(I32)
             )
         w1_right = load_weight("w1_right", w1, half, F)
+        gain = keep.tile([P, PACK], F32, name="gain")
+        nc.sync.dma_start(gain[:], gn.rearrange("(p t) o -> p (t o)", t=PACK))
         word_table = keep.tile([P, T], U32, name="word_table")
         nc.sync.dma_start(word_table[:].bitcast(I32), x_words[0].rearrange("p n t -> p (n t)").bitcast(I32))
-        gain = keep.tile([P, PACK], F32, name="gain")
-        nc.gpsimd.dma_start(gain[:], gn.rearrange("(p t) o -> p (t o)", t=PACK))
         n1_t = load_list("n1_t", n1)
         n2_t = load_list("n2_t", n2)
         w2_rows = load_weight("w2_rows", w2, 0, F)
@@ -99,9 +99,9 @@ def tile_picked_twlpathbhopmn_none_p_kernel(
         sign = keep.tile([P, PACK], F32, name="sign")
         twice = keep.tile([P, PACK], F32, name="twice")
         size = keep.tile([P, PACK], F32, name="size")
-        nc.vector.tensor_scalar(twice[:], gain[:], 0.0, 2.0, ALU.is_ge, ALU.mult)
-        nc.vector.tensor_scalar(sign[:], twice[:], -1.0, None, ALU.add)
-        nc.vector.tensor_tensor(size[:], gain[:], sign[:], ALU.mult)
+        nc.gpsimd.tensor_scalar(twice[:], gain[:], 0.0, 2.0, ALU.is_ge, ALU.mult)
+        nc.gpsimd.tensor_scalar(sign[:], twice[:], 1.0, -1.0, ALU.mult, ALU.add)
+        nc.vector.scalar_tensor_tensor(size[:], gain[:], -1.0, gain[:], ALU.mult, ALU.max)
 
         picked = []
         for name, lst in (("x_offs", offs_t), ("x_two", two_t)):
@@ -164,9 +164,9 @@ def tile_picked_twlpathbhopmn_none_p_kernel(
         for c0, c1 in Z_CHUNKS:
             grouped = keep.tile([P, PACK * (c1 - c0)], BF16, name="z_grouped%d" % c0, align_bytes=64)
             nc.vector.tensor_tensor(
-                grouped[:].rearrange("p (c i t) -> p c t i", i=4, t=PACK),
-                sum_a[:, :, c0:c1].rearrange("p t (c i) -> p c t i", i=4),
-                sum_b[:, :, c0:c1].rearrange("p t (c i) -> p c t i", i=4),
+                grouped[:].rearrange("p (c i t) -> p c t i", i=2, t=PACK),
+                sum_a[:, :, c0:c1].rearrange("p t (c i) -> p c t i", i=2),
+                sum_b[:, :, c0:c1].rearrange("p t (c i) -> p c t i", i=2),
                 ALU.max,
             )
             z_grouped.append(grouped)

@@ -42,24 +42,24 @@ def tile_picked_twlpathbhopmn_none_p_kernel(
 
         def deal(grouped, rows, m0, m1):
             nc.scalar.copy(
-                out=grouped[:].rearrange("p (t m j) -> p m t j", t=PACK, j=PACK)[:, m0:m1],
+                out=grouped.rearrange("p (t m j) -> p m t j", t=PACK, j=PACK)[:, m0:m1],
                 in_=rows.rearrange("p j (m t) -> p m t j", t=PACK),
             )
 
-        def quantise(name, grouped, width):
-            codes = keep.tile([P, width], U32, name=name + "_codes", align_bytes=64)
+        def quantise(name, grouped, width, tag=""):
+            codes = keep.tile([P, width], U32, name=name + "_codes", tag=tag, align_bytes=64)
             scales = keep.tile([P, width], U8, name=name + "_scales", align_bytes=64)
-            nc.vector.quantize_mx(out=codes[:].bitcast(FP8X4), scales=scales[:], in_=grouped[:])
+            nc.vector.quantize_mx(out=codes[:].bitcast(FP8X4), scales=scales[:], in_=grouped)
             return codes, scales
 
-        def product(acc, weight, t, moving):
+        def product(acc, weight, t, moving, c0, c1):
             cols = slice(P * t, P * (t + 1))
             nc.tensor.matmul_mx(
                 out=acc,
                 lhsT=weight[0][:, cols].bitcast(FP8X4),
                 lhsT_scale=weight[1][:, cols],
-                rhs=moving[0][:].bitcast(FP8X4),
-                rhs_scale=moving[1][:],
+                rhs=moving[0][:, c0:c1].bitcast(FP8X4),
+                rhs_scale=moving[1][:, c0:c1],
                 start=True,
                 stop=True,
             )
@@ -94,7 +94,7 @@ def tile_picked_twlpathbhopmn_none_p_kernel(
         for t in range(1, PACK):
             nc.scalar.activation(first[t][:, S:], first[0][:, S:], COPY)
         for t in range(PACK):
-            nc.vector.memset(second[t][:, S:], 0.0)
+            nc.gpsimd.memset(second[t][:, S:], 0.0)
 
         sign = keep.tile([P, PACK], F32, name="sign")
         twice = keep.tile([P, PACK], F32, name="twice")
@@ -110,25 +110,30 @@ def tile_picked_twlpathbhopmn_none_p_kernel(
             picked.append(scales)
 
         w1_grouped = keep.tile([P, PACK * F], BF16, name="w1_grouped", align_bytes=64)
-        deal(w1_grouped, w1_left[:], 0, 64)
-        deal(w1_grouped, w1_right[:], 64, 128)
-        w1_q = quantise("w1", w1_grouped, F)
+        deal(w1_grouped[:], w1_left[:], 0, 64)
+        deal(w1_grouped[:], w1_right[:], 64, 128)
+        w1_q = quantise("w1", w1_grouped[:], F)
 
+        halves = ((0, S // 2), (S // 2, S))
         tokens = []
-        for name, lst, scales in (("x_offs", offs_t, picked[0]), ("x_two", two_t, picked[1])):
+        for name, lst, scales, cuts in (("x_offs", offs_t, picked[0], halves), ("x_two", two_t, picked[1], ((0, S),))):
             words = keep.tile([P, S], U32, name=name + "_words", align_bytes=64)
-            nc.vector.tensor_copy(words[:], word_table[:].indirect(lst[:]))
+            for c0, c1 in cuts:
+                nc.vector.tensor_copy(words[:, c0:c1], word_table[:].indirect(lst[:, c0 // 16 : c1 // 16]))
             tokens.append((words, scales))
 
         banks = [psum.tile([P, S], F32, name="bank%d" % b) for b in range(2 * PACK)]
 
-        for t in range(PACK):
-            product(banks[t][:], w1_q, t, tokens[0])
+        for bank, (c0, c1) in zip((banks[PACK], banks[0]), halves):
+            product(bank[:, c0:c1], w1_q, 0, tokens[0], c0, c1)
+            nc.scalar.activation(first[0][:, c0:c1], bank[:, c0:c1], COPY, scale=size[:, 0:1])
+        for t in range(1, PACK):
+            product(banks[t][:], w1_q, t, tokens[0], 0, S)
             nc.scalar.activation(first[t][:, :S], banks[t][:], COPY, scale=size[:, t : t + 1])
 
         w2_grouped = keep.tile([P, PACK * F], BF16, name="w2_grouped", tag="w2_stage", align_bytes=64)
         for h in range(2):
-            deal(w2_grouped, w2_rows[:, :, half * h : half * (h + 1)], 64 * h, 64 * (h + 1))
+            deal(w2_grouped[:], w2_rows[:, :, half * h : half * (h + 1)], 64 * h, 64 * (h + 1))
 
         y_n1 = keep.tile([P, PACK, S], F32, name="y_n1")
         y_n2_early = keep.tile([P, 2, S], F32, name="y_n2_early")
@@ -136,50 +141,67 @@ def tile_picked_twlpathbhopmn_none_p_kernel(
             nc.vector.tensor_copy(y_n1[:, t, :], first[t][:].indirect(n1_t[:]))
             if t < 2:
                 nc.vector.tensor_copy(y_n2_early[:, t, :], first[t][:].indirect(n2_t[:]))
-        w2_q = quantise("w2", w2_grouped, F)
+        w2_q = quantise("w2", w2_grouped[:], F)
         y_n2_late = keep.tile([P, 2, S], F32, name="y_n2_late", tag="w2_stage", align_bytes=64)
         for t in range(2, PACK):
             nc.vector.tensor_copy(y_n2_late[:, t - 2, :], first[t][:].indirect(n2_t[:]))
         y_n2 = [y_n2_early[:, 0, :], y_n2_early[:, 1, :], y_n2_late[:, 0, :], y_n2_late[:, 1, :]]
 
-        for t in range(PACK):
-            product(banks[PACK + t][:], w2_q, t, tokens[1])
-            nc.scalar.activation(second[t][:, :S], banks[PACK + t][:], COPY, scale=size[:, t : t + 1])
-
         w3_signed = keep.tile([P, PACK, F], BF16, name="w3_signed")
         for j in range(PACK):
             nc.scalar.activation(w3_signed[:, j, :], w3_rows[:, j, :], COPY, scale=sign[:, j : j + 1])
-        w3_grouped = keep.tile([P, PACK * F], BF16, name="w3_grouped", align_bytes=64)
+
+        for t in range(PACK):
+            product(banks[PACK + t][:], w2_q, t, tokens[1], 0, S)
+            nc.scalar.activation(second[t][:, :S], banks[PACK + t][:], COPY, scale=size[:, t : t + 1])
+
+        shared0 = PACK * S - S // 2
+        shared = keep.tile([P, shared0 + PACK * F // 2], F32, name="shared", align_bytes=64)
+        sum_a = shared[:, : PACK * S].rearrange("p (t s) -> p t s", t=PACK)
+        w3_grouped = shared[:, shared0:].bitcast(BF16)
         for h in range(2):
             deal(w3_grouped, w3_signed[:, :, half * h : half * (h + 1)], 64 * h, 64 * (h + 1))
-
-        sum_a = keep.tile([P, PACK, S], F32, name="sum_a")
         sum_b = keep.tile([P, PACK, S], F32, name="sum_b")
-        for t in range(PACK):
-            nc.vector.tensor_tensor(sum_a[:, t, :], second[t][:].indirect(n3_t[:]), y_n1[:, t, :], ALU.add)
-            nc.vector.tensor_tensor(sum_b[:, t, :], second[t][:].indirect(n4_t[:]), y_n2[t], ALU.add)
-        w3_q = quantise("w3", w3_grouped, F)
 
-        z_grouped = []
-        for c0, c1 in Z_CHUNKS:
-            grouped = keep.tile([P, PACK * (c1 - c0)], BF16, name="z_grouped%d" % c0, align_bytes=64)
+        def add_pair(t, c0, c1):
+            lists = slice(c0 // 16, c1 // 16)
+            nc.vector.tensor_tensor(
+                sum_a[:, t, c0:c1], second[t][:].indirect(n3_t[:, lists]), y_n1[:, t, c0:c1], ALU.add
+            )
+            nc.vector.tensor_tensor(
+                sum_b[:, t, c0:c1], second[t][:].indirect(n4_t[:, lists]), y_n2[t][:, c0:c1], ALU.add
+            )
+
+        def larger(c0, c1):
+            grouped = keep.tile([P, PACK * (c1 - c0)], BF16, name="z_grouped%d" % c0, tag="z%d" % c0, align_bytes=64)
             nc.vector.tensor_tensor(
                 grouped[:].rearrange("p (c i t) -> p c t i", i=2, t=PACK),
                 sum_a[:, :, c0:c1].rearrange("p t (c i) -> p c t i", i=2),
                 sum_b[:, :, c0:c1].rearrange("p t (c i) -> p c t i", i=2),
                 ALU.max,
             )
-            z_grouped.append(grouped)
-        last0 = Z_CHUNKS[-1][0]
-        for grouped, (c0, c1) in zip(z_grouped, Z_CHUNKS):
-            z_q = quantise("z%d" % c0, grouped, c1 - c0)
-            for t in range(PACK):
-                bank = banks[t] if c0 < last0 else banks[PACK + t]
-                product(bank[:, c0:c1], w3_q, t, z_q)
-                if c1 == last0:
-                    nc.scalar.copy(first[t][:, :last0], bank[:, :last0])
-                if c0 == last0:
-                    nc.scalar.copy(first[t][:, last0:S], bank[:, last0:S])
+            return grouped
+
+        for t in range(PACK - 1):
+            add_pair(t, 0, S)
+        add_pair(PACK - 1, 0, S // 2)
+        z_grouped = [larger(*Z_CHUNKS[0])]
+        w3_first = quantise("w3_first", w3_grouped[:, :F], P)
+        z_q = [quantise("z0", z_grouped[0][:], S // 2)]
+        add_pair(PACK - 1, S // 2, S)
+        z_grouped += [larger(c0, c1) for c0, c1 in Z_CHUNKS[1:]]
+        z_q += [quantise("z%d" % c0, g[:], c1 - c0) for g, (c0, c1) in zip(z_grouped[1:], Z_CHUNKS[1:])]
+
+        w3_second = quantise("w3_second", w3_grouped[:, F : 2 * F], P, tag="z%d" % Z_CHUNKS[1][0])
+        w3_rest = quantise("w3_rest", w3_grouped[:, 2 * F :], 2 * P, tag="z%d" % Z_CHUNKS[2][0])
+
+        for n, (c0, c1) in enumerate(Z_CHUNKS):
+            product(banks[n][:, c0:c1], w3_first, 0, z_q[n], 0, c1 - c0)
+            nc.scalar.copy(first[0][:, c0:c1], banks[n][:, c0:c1])
+        for t, weight, column in ((1, w3_second, 0), (2, w3_rest, 0), (3, w3_rest, 1)):
+            for n, (c0, c1) in enumerate(Z_CHUNKS):
+                product(banks[PACK + t][:, c0:c1], weight, column, z_q[n], 0, c1 - c0)
+            nc.scalar.copy(first[t][:, :S], banks[PACK + t][:])
 
         out_rows = out.rearrange("(p t) j -> p t j", t=PACK)
         h_n5 = [keep.tile([P, S], F32, name="h_n5_%d" % t) for t in range(PACK)]

@@ -17,8 +17,11 @@ PACK = 4
 T = 2048
 S = 512
 F = 512
+STRIPE = 16
+QUADRANT = 32
 WINDOW = 2 * S
-Z_CHUNKS = ((0, 256), (256, 384), (384, 512))
+HALVES = ((0, S // 2), (S // 2, S))
+Z_CHUNKS = ((0, S // 2), (S // 2, 3 * S // 4), (3 * S // 4, S))
 FLOPS = 3 * 2 * F * F * S
 
 
@@ -31,18 +34,21 @@ def tile_picked_twlpathbhopmn_none_p_kernel(
         psum = ctx.enter_context(tc.psum_pool(name="psum", bufs=1))
 
         def load_list(name, source):
-            tile = keep.tile([P, S // 16], U16, name=name)
+            tile = keep.tile([P, S // STRIPE], U16, name=name)
             nc.sync.dma_start(tile[:], source)
             return tile
+
+        def entries(list_tile, c0, c1):
+            return list_tile[:, c0 // STRIPE : c1 // STRIPE]
 
         def load_weight(name, source, c0, c1):
             tile = keep.tile([P, PACK, c1 - c0], F32, name=name)
             nc.sync.dma_start(tile[:], source.rearrange("(p j) c -> p j c", j=PACK)[:, :, c0:c1])
             return tile
 
-        def deal(grouped, rows, m0, m1):
+        def deal(grouped, rows, c0, c1):
             nc.scalar.copy(
-                out=grouped.rearrange("p (t m j) -> p m t j", t=PACK, j=PACK)[:, m0:m1],
+                out=grouped.rearrange("p (t m j) -> p m t j", t=PACK, j=PACK)[:, c0 // PACK : c1 // PACK],
                 in_=rows.rearrange("p j (m t) -> p m t j", t=PACK),
             )
 
@@ -52,8 +58,8 @@ def tile_picked_twlpathbhopmn_none_p_kernel(
             nc.vector.quantize_mx(out=codes[:].bitcast(FP8X4), scales=scales[:], in_=grouped)
             return codes, scales
 
-        def product(acc, weight, t, moving, c0, c1):
-            cols = slice(P * t, P * (t + 1))
+        def product(acc, weight, block, moving, c0, c1):
+            cols = slice(P * block, P * (block + 1))
             nc.tensor.matmul_mx(
                 out=acc,
                 lhsT=weight[0][:, cols].bitcast(FP8X4),
@@ -68,13 +74,13 @@ def tile_picked_twlpathbhopmn_none_p_kernel(
         nc.vector.memset(scale_table[:].bitcast(I32), 0)
         offs_t = load_list("offs_t", offs)
         two_t = load_list("two_t", two)
-        half = F // 2
-        w1_left = load_weight("w1_left", w1, 0, half)
-        for q in range(4):
+        w1_left = load_weight("w1_left", w1, 0, F // 2)
+        for q in range(P // QUADRANT):
             nc.sync.dma_start(
-                scale_table[32 * q : 32 * q + 4, :].bitcast(I32), x_scales[0, 4 * q : 4 * q + 4, :].bitcast(I32)
+                scale_table[QUADRANT * q : QUADRANT * q + 4, :].bitcast(I32),
+                x_scales[0, 4 * q : 4 * q + 4, :].bitcast(I32),
             )
-        w1_right = load_weight("w1_right", w1, half, F)
+        w1_right = load_weight("w1_right", w1, F // 2, F)
         gain = keep.tile([P, PACK], F32, name="gain")
         nc.sync.dma_start(gain[:], gn.rearrange("(p t) o -> p (t o)", t=PACK))
         word_table = keep.tile([P, T], U32, name="word_table")
@@ -90,9 +96,9 @@ def tile_picked_twlpathbhopmn_none_p_kernel(
 
         first = [keep.tile([P, WINDOW], F32, name="first%d" % t) for t in range(PACK)]
         second = [keep.tile([P, WINDOW], F32, name="second%d" % t) for t in range(PACK)]
-        nc.vector.memset(first[0][:, S:], 0.0)
-        for t in range(1, PACK):
-            nc.scalar.activation(first[t][:, S:], first[0][:, S:], COPY)
+        for t in range(PACK - 1):
+            nc.vector.memset(first[t][:, S:], 0.0)
+        nc.scalar.activation(first[PACK - 1][:, S:], first[0][:, S:], COPY)
         for t in range(PACK):
             nc.gpsimd.memset(second[t][:, S:], 0.0)
 
@@ -103,73 +109,72 @@ def tile_picked_twlpathbhopmn_none_p_kernel(
         nc.gpsimd.tensor_scalar(sign[:], twice[:], 1.0, -1.0, ALU.mult, ALU.add)
         nc.vector.scalar_tensor_tensor(size[:], gain[:], -1.0, gain[:], ALU.mult, ALU.max)
 
-        picked = []
-        for name, lst in (("x_offs", offs_t), ("x_two", two_t)):
-            scales = keep.tile([P, S], U8, name=name + "_scales", align_bytes=64)
-            nc.vector.tensor_copy(scales[:], scale_table[:].indirect(lst[:]))
-            picked.append(scales)
+        offs_scales = keep.tile([P, S], U8, name="offs_scales", align_bytes=64)
+        nc.vector.tensor_copy(offs_scales[:], scale_table[:].indirect(offs_t[:]))
+        two_scales = keep.tile([P, S], U8, name="two_scales", align_bytes=64)
+        nc.vector.tensor_copy(two_scales[:], scale_table[:].indirect(two_t[:]))
 
         w1_grouped = keep.tile([P, PACK * F], BF16, name="w1_grouped", align_bytes=64)
-        deal(w1_grouped[:], w1_left[:], 0, 64)
-        deal(w1_grouped[:], w1_right[:], 64, 128)
+        deal(w1_grouped[:], w1_left[:], 0, F // 2)
+        deal(w1_grouped[:], w1_right[:], F // 2, F)
         w1_q = quantise("w1", w1_grouped[:], F)
 
-        halves = ((0, S // 2), (S // 2, S))
-        tokens = []
-        for name, lst, scales, cuts in (("x_offs", offs_t, picked[0], halves), ("x_two", two_t, picked[1], ((0, S),))):
-            words = keep.tile([P, S], U32, name=name + "_words", align_bytes=64)
-            for c0, c1 in cuts:
-                nc.vector.tensor_copy(words[:, c0:c1], word_table[:].indirect(lst[:, c0 // 16 : c1 // 16]))
-            tokens.append((words, scales))
+        offs_words = keep.tile([P, S], U32, name="offs_words", align_bytes=64)
+        for c0, c1 in HALVES:
+            nc.vector.tensor_copy(offs_words[:, c0:c1], word_table[:].indirect(entries(offs_t, c0, c1)))
+        two_words = keep.tile([P, S], U32, name="two_words", align_bytes=64)
+        nc.vector.tensor_copy(two_words[:], word_table[:].indirect(two_t[:]))
+        x_offs = (offs_words, offs_scales)
+        x_two = (two_words, two_scales)
 
         banks = [psum.tile([P, S], F32, name="bank%d" % b) for b in range(2 * PACK)]
 
-        for bank, (c0, c1) in zip((banks[PACK], banks[0]), halves):
-            product(bank[:, c0:c1], w1_q, 0, tokens[0], c0, c1)
+        for bank, (c0, c1) in zip((banks[PACK], banks[0]), HALVES):
+            product(bank[:, c0:c1], w1_q, 0, x_offs, c0, c1)
             nc.scalar.activation(first[0][:, c0:c1], bank[:, c0:c1], COPY, scale=size[:, 0:1])
         for t in range(1, PACK):
-            product(banks[t][:], w1_q, t, tokens[0], 0, S)
+            product(banks[t][:], w1_q, t, x_offs, 0, S)
             nc.scalar.activation(first[t][:, :S], banks[t][:], COPY, scale=size[:, t : t + 1])
 
         w2_grouped = keep.tile([P, PACK * F], BF16, name="w2_grouped", tag="w2_stage", align_bytes=64)
-        for h in range(2):
-            deal(w2_grouped[:], w2_rows[:, :, half * h : half * (h + 1)], 64 * h, 64 * (h + 1))
+        for c0, c1 in HALVES:
+            deal(w2_grouped[:], w2_rows[:, :, c0:c1], c0, c1)
 
+        early = PACK // 2
         y_n1 = keep.tile([P, PACK, S], F32, name="y_n1")
-        y_n2_early = keep.tile([P, 2, S], F32, name="y_n2_early")
+        y_n2_early = keep.tile([P, early, S], F32, name="y_n2_early")
         for t in range(PACK):
             nc.vector.tensor_copy(y_n1[:, t, :], first[t][:].indirect(n1_t[:]))
-            if t < 2:
+            if t < early:
                 nc.vector.tensor_copy(y_n2_early[:, t, :], first[t][:].indirect(n2_t[:]))
         w2_q = quantise("w2", w2_grouped[:], F)
-        y_n2_late = keep.tile([P, 2, S], F32, name="y_n2_late", tag="w2_stage", align_bytes=64)
-        for t in range(2, PACK):
-            nc.vector.tensor_copy(y_n2_late[:, t - 2, :], first[t][:].indirect(n2_t[:]))
-        y_n2 = [y_n2_early[:, 0, :], y_n2_early[:, 1, :], y_n2_late[:, 0, :], y_n2_late[:, 1, :]]
+        y_n2_late = keep.tile([P, PACK - early, S], F32, name="y_n2_late", tag="w2_stage", align_bytes=64)
+        for t in range(early, PACK):
+            nc.vector.tensor_copy(y_n2_late[:, t - early, :], first[t][:].indirect(n2_t[:]))
+        y_n2 = [y_n2_early[:, t, :] if t < early else y_n2_late[:, t - early, :] for t in range(PACK)]
 
         w3_signed = keep.tile([P, PACK, F], BF16, name="w3_signed")
         for j in range(PACK):
             nc.scalar.activation(w3_signed[:, j, :], w3_rows[:, j, :], COPY, scale=sign[:, j : j + 1])
 
         for t in range(PACK):
-            product(banks[PACK + t][:], w2_q, t, tokens[1], 0, S)
+            product(banks[PACK + t][:], w2_q, t, x_two, 0, S)
             nc.scalar.activation(second[t][:, :S], banks[PACK + t][:], COPY, scale=size[:, t : t + 1])
 
-        shared0 = PACK * S - S // 2
-        shared = keep.tile([P, shared0 + PACK * F // 2], F32, name="shared", align_bytes=64)
+        w3_start = PACK * S - S // 2
+        shared = keep.tile([P, w3_start + PACK * F // 2], F32, name="shared", align_bytes=64)
         sum_a = shared[:, : PACK * S].rearrange("p (t s) -> p t s", t=PACK)
-        w3_grouped = shared[:, shared0:].bitcast(BF16)
-        for h in range(2):
-            deal(w3_grouped, w3_signed[:, :, half * h : half * (h + 1)], 64 * h, 64 * (h + 1))
+        w3_grouped = shared[:, w3_start:].bitcast(BF16)
+        for c0, c1 in HALVES:
+            deal(w3_grouped, w3_signed[:, :, c0:c1], c0, c1)
         sum_b = keep.tile([P, PACK, S], F32, name="sum_b")
 
         def add_pair(t, c0, c1):
-            lists = slice(c0 // 16, c1 // 16)
             nc.vector.tensor_tensor(
-                sum_a[:, t, c0:c1], second[t][:].indirect(n3_t[:, lists]), y_n1[:, t, c0:c1], ALU.add
+                sum_a[:, t, c0:c1], second[t][:].indirect(entries(n3_t, c0, c1)), y_n1[:, t, c0:c1], ALU.add
             )
             nc.vector.tensor_tensor(
-                sum_b[:, t, c0:c1], second[t][:].indirect(n4_t[:, lists]), y_n2[t][:, c0:c1], ALU.add
+                sum_b[:, t, c0:c1], second[t][:].indirect(entries(n4_t, c0, c1)), y_n2[t][:, c0:c1], ALU.add
             )
 
         def larger(c0, c1):
@@ -184,11 +189,11 @@ def tile_picked_twlpathbhopmn_none_p_kernel(
 
         for t in range(PACK - 1):
             add_pair(t, 0, S)
-        add_pair(PACK - 1, 0, S // 2)
+        add_pair(PACK - 1, *HALVES[0])
         z_grouped = [larger(*Z_CHUNKS[0])]
         w3_first = quantise("w3_first", w3_grouped[:, :F], P)
         z_q = [quantise("z0", z_grouped[0][:], S // 2)]
-        add_pair(PACK - 1, S // 2, S)
+        add_pair(PACK - 1, *HALVES[1])
         z_grouped += [larger(c0, c1) for c0, c1 in Z_CHUNKS[1:]]
         z_q += [quantise("z%d" % c0, g[:], c1 - c0) for g, (c0, c1) in zip(z_grouped[1:], Z_CHUNKS[1:])]
 
@@ -198,30 +203,36 @@ def tile_picked_twlpathbhopmn_none_p_kernel(
         for n, (c0, c1) in enumerate(Z_CHUNKS):
             product(banks[n][:, c0:c1], w3_first, 0, z_q[n], 0, c1 - c0)
             nc.scalar.copy(first[0][:, c0:c1], banks[n][:, c0:c1])
-        for t, weight, column in ((1, w3_second, 0), (2, w3_rest, 0), (3, w3_rest, 1)):
+        for t, weight, block in ((1, w3_second, 0), (2, w3_rest, 0), (3, w3_rest, 1)):
             for n, (c0, c1) in enumerate(Z_CHUNKS):
-                product(banks[PACK + t][:, c0:c1], weight, column, z_q[n], 0, c1 - c0)
+                product(banks[PACK + t][:, c0:c1], weight, block, z_q[n], 0, c1 - c0)
             nc.scalar.copy(first[t][:, :S], banks[PACK + t][:])
 
         out_rows = out.rearrange("(p t) j -> p t j", t=PACK)
         h_n5 = [keep.tile([P, S], F32, name="h_n5_%d" % t) for t in range(PACK)]
+
+        def make_st(t):
+            nc.vector.tensor_tensor(second[t][:, :S], h_n5[t][:], first[t][:, :S], ALU.max)
+
+        def fetch_st(t, c0, c1):
+            st_n6 = keep.tile([P, c1 - c0], F32, name="st_n6_%d_%d" % (t, c0))
+            nc.vector.tensor_copy(st_n6[:], second[t][:].indirect(entries(n6_t, c0, c1)))
+            return st_n6
+
+        def store_smaller(st_n6, t, c0, c1):
+            result = keep.tile([P, c1 - c0], F32, name="result%d_%d" % (t, c0))
+            nc.vector.tensor_tensor(result[:], st_n6[:], second[t][:, c0:c1], ALU.min)
+            nc.sync.dma_start(out_rows[:, t, c0:c1], result[:])
+
         for t in range(PACK):
             nc.vector.tensor_copy(h_n5[t][:], first[t][:].indirect(n5_t[:]))
             if t > 0:
-                nc.vector.tensor_tensor(second[t - 1][:, :S], h_n5[t - 1][:], first[t - 1][:, :S], ALU.max)
-        pieces = [(t, 0, S) for t in range(PACK - 1)] + [(PACK - 1, 0, S // 2), (PACK - 1, S // 2, S)]
-        fetched = []
-        for n, (t, c0, c1) in enumerate(pieces):
-            st_n6 = keep.tile([P, c1 - c0], F32, name="st_n6_%d" % n)
-            nc.vector.tensor_copy(st_n6[:], second[t][:].indirect(n6_t[:, c0 // 16 : c1 // 16]))
-            fetched.append(st_n6)
-            if n == 0:
-                nc.vector.tensor_tensor(second[PACK - 1][:, :S], h_n5[PACK - 1][:], first[PACK - 1][:, :S], ALU.max)
-            todo = [n - 1] if n > 0 else []
-            if n == len(pieces) - 1:
-                todo.append(n)
-            for k in todo:
-                tk, k0, k1 = pieces[k]
-                result = keep.tile([P, k1 - k0], F32, name="result%d" % k)
-                nc.vector.tensor_tensor(result[:], fetched[k][:], second[tk][:, k0:k1], ALU.min)
-                nc.sync.dma_start(out_rows[:, tk, k0:k1], result[:])
+                make_st(t - 1)
+        pieces = [(t, 0, S) for t in range(PACK - 1)] + [(PACK - 1, c0, c1) for c0, c1 in HALVES]
+        waiting = fetch_st(*pieces[0])
+        make_st(PACK - 1)
+        for before, piece in zip(pieces, pieces[1:]):
+            fetched = fetch_st(*piece)
+            store_smaller(waiting, *before)
+            waiting = fetched
+        store_smaller(waiting, *pieces[-1])

from contextlib import ExitStack

import concourse.mybir as mybir

F32 = mybir.dt.float32
BF16 = mybir.dt.bfloat16
I32 = mybir.dt.int32
U32 = mybir.dt.uint32
U16 = mybir.dt.uint16
U8 = mybir.dt.uint8
FP8X4 = mybir.dt.float8_e4m3fn_x4
ALU = mybir.AluOpType
COPY = mybir.ActivationFunctionType.Copy

P = 128
PACK = 4
T = 2048
S = 512
F = 512
STRIPE = 16
QUADRANT = 32
WINDOW = 2 * S
HALVES = ((0, S // 2), (S // 2, S))
Z_CHUNKS = ((0, S // 2), (S // 2, 3 * S // 4), (3 * S // 4, S))
FLOPS = 3 * 2 * F * F * S


def tile_picked_twlpathbhopmn_none_p_kernel(
    tc, x_words, x_scales, w1, w2, gn, w3, offs, two, n1, n2, n3, n4, n5, n6, out
):
    nc = tc.nc
    with ExitStack() as ctx:
        keep = ctx.enter_context(tc.tile_pool(name="keep", bufs=1))
        psum = ctx.enter_context(tc.psum_pool(name="psum", bufs=1))

        def load_list(name, source):
            tile = keep.tile([P, S // STRIPE], U16, name=name)
            nc.sync.dma_start(tile[:], source)
            return tile

        def entries(list_tile, c0, c1):
            return list_tile[:, c0 // STRIPE : c1 // STRIPE]

        def load_weight(name, source, c0, c1):
            tile = keep.tile([P, PACK, c1 - c0], F32, name=name)
            nc.sync.dma_start(tile[:], source.rearrange("(p j) c -> p j c", j=PACK)[:, :, c0:c1])
            return tile

        def deal(grouped, rows, c0, c1):
            nc.scalar.copy(
                out=grouped.rearrange("p (t m j) -> p m t j", t=PACK, j=PACK)[:, c0 // PACK : c1 // PACK],
                in_=rows.rearrange("p j (m t) -> p m t j", t=PACK),
            )

        def quantise(name, grouped, width, tag=""):
            codes = keep.tile([P, width], U32, name=name + "_codes", tag=tag, align_bytes=64)
            scales = keep.tile([P, width], U8, name=name + "_scales", align_bytes=64)
            nc.vector.quantize_mx(out=codes[:].bitcast(FP8X4), scales=scales[:], in_=grouped)
            return codes, scales

        def product(acc, weight, block, moving, c0, c1):
            cols = slice(P * block, P * (block + 1))
            nc.tensor.matmul_mx(
                out=acc,
                lhsT=weight[0][:, cols].bitcast(FP8X4),
                lhsT_scale=weight[1][:, cols],
                rhs=moving[0][:, c0:c1].bitcast(FP8X4),
                rhs_scale=moving[1][:, c0:c1],
                start=True,
                stop=True,
            )

        scale_table = keep.tile([P, T], U8, name="scale_table")
        nc.vector.memset(scale_table[:].bitcast(I32), 0)
        offs_t = load_list("offs_t", offs)
        two_t = load_list("two_t", two)
        w1_left = load_weight("w1_left", w1, 0, F // 2)
        for q in range(P // QUADRANT):
            nc.sync.dma_start(
                scale_table[QUADRANT * q : QUADRANT * q + 4, :].bitcast(I32),
                x_scales[0, 4 * q : 4 * q + 4, :].bitcast(I32),
            )
        w1_right = load_weight("w1_right", w1, F // 2, F)
        gain = keep.tile([P, PACK], F32, name="gain")
        nc.sync.dma_start(gain[:], gn.rearrange("(p t) o -> p (t o)", t=PACK))
        word_table = keep.tile([P, T], U32, name="word_table")
        nc.sync.dma_start(word_table[:].bitcast(I32), x_words[0].rearrange("p n t -> p (n t)").bitcast(I32))
        n1_t = load_list("n1_t", n1)
        n2_t = load_list("n2_t", n2)
        w2_rows = load_weight("w2_rows", w2, 0, F)
        n3_t = load_list("n3_t", n3)
        n4_t = load_list("n4_t", n4)
        w3_rows = load_weight("w3_rows", w3, 0, F)
        n5_t = load_list("n5_t", n5)
        n6_t = load_list("n6_t", n6)

        first = [keep.tile([P, WINDOW], F32, name="first%d" % t) for t in range(PACK)]
        second = [keep.tile([P, WINDOW], F32, name="second%d" % t) for t in range(PACK)]
        for t in range(PACK - 1):
            nc.vector.memset(first[t][:, S:], 0.0)
        nc.scalar.activation(first[PACK - 1][:, S:], first[0][:, S:], COPY)
        for t in range(PACK):
            nc.gpsimd.memset(second[t][:, S:], 0.0)

        sign = keep.tile([P, PACK], F32, name="sign")
        twice = keep.tile([P, PACK], F32, name="twice")
        size = keep.tile([P, PACK], F32, name="size")
        nc.gpsimd.tensor_scalar(twice[:], gain[:], 0.0, 2.0, ALU.is_ge, ALU.mult)
        nc.gpsimd.tensor_scalar(sign[:], twice[:], 1.0, -1.0, ALU.mult, ALU.add)
        nc.vector.scalar_tensor_tensor(size[:], gain[:], -1.0, gain[:], ALU.mult, ALU.max)

        offs_scales = keep.tile([P, S], U8, name="offs_scales", align_bytes=64)
        nc.vector.tensor_copy(offs_scales[:], scale_table[:].indirect(offs_t[:]))
        two_scales = keep.tile([P, S], U8, name="two_scales", align_bytes=64)
        nc.vector.tensor_copy(two_scales[:], scale_table[:].indirect(two_t[:]))

        w1_grouped = keep.tile([P, PACK * F], BF16, name="w1_grouped", align_bytes=64)
        deal(w1_grouped[:], w1_left[:], 0, F // 2)
        deal(w1_grouped[:], w1_right[:], F // 2, F)
        w1_q = quantise("w1", w1_grouped[:], F)

        offs_words = keep.tile([P, S], U32, name="offs_words", align_bytes=64)
        for c0, c1 in HALVES:
            nc.vector.tensor_copy(offs_words[:, c0:c1], word_table[:].indirect(entries(offs_t, c0, c1)))
        two_words = keep.tile([P, S], U32, name="two_words", align_bytes=64)
        nc.vector.tensor_copy(two_words[:], word_table[:].indirect(two_t[:]))
        x_offs = (offs_words, offs_scales)
        x_two = (two_words, two_scales)

        banks = [psum.tile([P, S], F32, name="bank%d" % b) for b in range(2 * PACK)]

        for bank, (c0, c1) in zip((banks[PACK], banks[0]), HALVES):
            product(bank[:, c0:c1], w1_q, 0, x_offs, c0, c1)
            nc.scalar.activation(first[0][:, c0:c1], bank[:, c0:c1], COPY, scale=size[:, 0:1])
        for t in range(1, PACK):
            product(banks[t][:], w1_q, t, x_offs, 0, S)
            nc.scalar.activation(first[t][:, :S], banks[t][:], COPY, scale=size[:, t : t + 1])

        w2_grouped = keep.tile([P, PACK * F], BF16, name="w2_grouped", tag="w2_stage", align_bytes=64)
        for c0, c1 in HALVES:
            deal(w2_grouped[:], w2_rows[:, :, c0:c1], c0, c1)

        early = PACK // 2
        y_n1 = keep.tile([P, PACK, S], F32, name="y_n1")
        y_n2_early = keep.tile([P, early, S], F32, name="y_n2_early")
        for t in range(PACK):
            nc.vector.tensor_copy(y_n1[:, t, :], first[t][:].indirect(n1_t[:]))
            if t < early:
                nc.vector.tensor_copy(y_n2_early[:, t, :], first[t][:].indirect(n2_t[:]))
        w2_q = quantise("w2", w2_grouped[:], F)
        y_n2_late = keep.tile([P, PACK - early, S], F32, name="y_n2_late", tag="w2_stage", align_bytes=64)
        for t in range(early, PACK):
            nc.vector.tensor_copy(y_n2_late[:, t - early, :], first[t][:].indirect(n2_t[:]))
        y_n2 = [y_n2_early[:, t, :] if t < early else y_n2_late[:, t - early, :] for t in range(PACK)]

        w3_signed = keep.tile([P, PACK, F], BF16, name="w3_signed")
        for j in range(PACK):
            nc.scalar.activation(w3_signed[:, j, :], w3_rows[:, j, :], COPY, scale=sign[:, j : j + 1])

        for t in range(PACK):
            product(banks[PACK + t][:], w2_q, t, x_two, 0, S)
            nc.scalar.activation(second[t][:, :S], banks[PACK + t][:], COPY, scale=size[:, t : t + 1])

        w3_start = PACK * S - S // 2
        shared = keep.tile([P, w3_start + PACK * F // 2], F32, name="shared", align_bytes=64)
        sum_a = shared[:, : PACK * S].rearrange("p (t s) -> p t s", t=PACK)
        w3_grouped = shared[:, w3_start:].bitcast(BF16)
        for c0, c1 in HALVES:
            deal(w3_grouped, w3_signed[:, :, c0:c1], c0, c1)
        sum_b = keep.tile([P, PACK, S], F32, name="sum_b")

        def add_pair(t, c0, c1):
            nc.vector.tensor_tensor(
                sum_a[:, t, c0:c1], second[t][:].indirect(entries(n3_t, c0, c1)), y_n1[:, t, c0:c1], ALU.add
            )
            nc.vector.tensor_tensor(
                sum_b[:, t, c0:c1], second[t][:].indirect(entries(n4_t, c0, c1)), y_n2[t][:, c0:c1], ALU.add
            )

        def larger(c0, c1):
            grouped = keep.tile([P, PACK * (c1 - c0)], BF16, name="z_grouped%d" % c0, tag="z%d" % c0, align_bytes=64)
            nc.vector.tensor_tensor(
                grouped[:].rearrange("p (c i t) -> p c t i", i=2, t=PACK),
                sum_a[:, :, c0:c1].rearrange("p t (c i) -> p c t i", i=2),
                sum_b[:, :, c0:c1].rearrange("p t (c i) -> p c t i", i=2),
                ALU.max,
            )
            return grouped

        for t in range(PACK - 1):
            add_pair(t, 0, S)
        add_pair(PACK - 1, *HALVES[0])
        z_grouped = [larger(*Z_CHUNKS[0])]
        w3_first = quantise("w3_first", w3_grouped[:, :F], P)
        z_q = [quantise("z0", z_grouped[0][:], S // 2)]
        add_pair(PACK - 1, *HALVES[1])
        z_grouped += [larger(c0, c1) for c0, c1 in Z_CHUNKS[1:]]
        z_q += [quantise("z%d" % c0, g[:], c1 - c0) for g, (c0, c1) in zip(z_grouped[1:], Z_CHUNKS[1:])]

        w3_second = quantise("w3_second", w3_grouped[:, F : 2 * F], P, tag="z%d" % Z_CHUNKS[1][0])
        w3_rest = quantise("w3_rest", w3_grouped[:, 2 * F :], 2 * P, tag="z%d" % Z_CHUNKS[2][0])

        for n, (c0, c1) in enumerate(Z_CHUNKS):
            product(banks[n][:, c0:c1], w3_first, 0, z_q[n], 0, c1 - c0)
            nc.scalar.copy(first[0][:, c0:c1], banks[n][:, c0:c1])
        for t, weight, block in ((1, w3_second, 0), (2, w3_rest, 0), (3, w3_rest, 1)):
            for n, (c0, c1) in enumerate(Z_CHUNKS):
                product(banks[PACK + t][:, c0:c1], weight, block, z_q[n], 0, c1 - c0)
            nc.scalar.copy(first[t][:, :S], banks[PACK + t][:])

        out_rows = out.rearrange("(p t) j -> p t j", t=PACK)
        h_n5 = [keep.tile([P, S], F32, name="h_n5_%d" % t) for t in range(PACK)]

        def make_st(t):
            nc.vector.tensor_tensor(second[t][:, :S], h_n5[t][:], first[t][:, :S], ALU.max)

        def fetch_st(t, c0, c1):
            st_n6 = keep.tile([P, c1 - c0], F32, name="st_n6_%d_%d" % (t, c0))
            nc.vector.tensor_copy(st_n6[:], second[t][:].indirect(entries(n6_t, c0, c1)))
            return st_n6

        def store_smaller(st_n6, t, c0, c1):
            result = keep.tile([P, c1 - c0], F32, name="result%d_%d" % (t, c0))
            nc.vector.tensor_tensor(result[:], st_n6[:], second[t][:, c0:c1], ALU.min)
            nc.sync.dma_start(out_rows[:, t, c0:c1], result[:])

        for t in range(PACK):
            nc.vector.tensor_copy(h_n5[t][:], first[t][:].indirect(n5_t[:]))
            if t > 0:
                make_st(t - 1)
        pieces = [(t, 0, S) for t in range(PACK - 1)] + [(PACK - 1, c0, c1) for c0, c1 in HALVES]
        waiting = fetch_st(*pieces[0])
        make_st(PACK - 1)
        for before, piece in zip(pieces, pieces[1:]):
            fetched = fetch_st(*piece)
            store_smaller(waiting, *before)
            waiting = fetched
        store_smaller(waiting, *pieces[-1])
